import numpy as np
import ml_dtypes


def mxq(x, axis, fmt="e4m3"):
    dtype, down = {"e4m3": (ml_dtypes.float8_e4m3fn, 7), "e5m2": (ml_dtypes.float8_e5m2, 14)}[fmt]
    v = np.moveaxis(np.asarray(x, np.float32).astype(ml_dtypes.bfloat16).astype(np.float64), axis, -1)
    blocks = v.reshape(v.shape[:-1] + (-1, 32))
    amax = np.abs(blocks).max(-1, keepdims=True)
    byte = np.maximum(np.where(amax > 0, np.frexp(amax)[1] - 1 + 127, 0) - down, 1)
    scale = np.exp2(byte - 127.0)
    codes = (blocks / scale).astype(np.float32).astype(dtype).astype(np.float64)
    return np.moveaxis((codes * scale).reshape(v.shape), -1, axis)


WIDE = False


def mx_kscale(k):
    if not WIDE:
        return np.ones(k)
    levels = np.array([10, -10, 5, -5, 0])
    if k % 512:
        return np.exp2(np.random.permutation(np.resize(levels, k // 32))).repeat(32)
    a = np.empty((k // 512, 16))
    for p in range(k // 512):
        a[p, :8] = np.random.permutation(np.resize(levels, 8))
        for g in range(8):
            far = levels[np.abs(levels - a[p, g]) >= 10]
            a[p, g + 8] = far[np.random.randint(len(far))]
    return np.exp2(a.ravel()).repeat(32)


def f64(x):
    return np.asarray(x).astype(np.float64)


def striped(idx):
    return np.tile(idx.reshape(-1, 16).T, (8, 1)).astype(np.uint16)


def unstriped(offs):
    return offs[:16].T.reshape(-1).astype(np.int64)


def striped8(idx):
    return np.concatenate([x.reshape(-1, 16).T for x in idx]).astype(np.uint16)


def runs(offs, k):
    lists = np.stack([offs[16 * r : 16 * r + 16].T.reshape(-1) for r in range(8)]).astype(np.int64)
    return lists[np.arange(k) % 512 // 64]


def pack_weight(w):
    k, n = w.shape
    w = f64(np.asarray(w, np.float32).astype(ml_dtypes.bfloat16)).reshape(k // 32, 32, n)
    amax = np.abs(w).max(1)
    byte = np.clip(np.where(amax > 0, np.frexp(amax)[1] - 1 + 127 - 7, 1), 1, 254)
    scaled = (w * np.exp2(127.0 - byte)[:, None, :]).reshape(k, n).astype(np.float32)
    words = np.ascontiguousarray(scaled.reshape(k // 512, 128, 4, n).transpose(0, 1, 3, 2)).astype(ml_dtypes.float8_e4m3fn).view(np.uint8)
    return words, np.ascontiguousarray(byte.astype(np.uint8).reshape(k // 512, 16, n))


def unpack_weight(words, scales):
    g, p, n, _ = words.shape
    vals = np.ascontiguousarray(words).view(ml_dtypes.float8_e4m3fn).astype(np.float64) * np.repeat(np.exp2(scales.astype(np.float64) - 127.0), 8, axis=1)[..., None]
    return vals.transpose(0, 1, 3, 2).reshape(g * 512, n)


K, T, S, N, H, J, C = 512, 2048, 512, 512, 512, 512, 512


def setup_inputs():
    n = np.random.standard_normal
    s = mx_kscale(K)[:, None]
    u = mx_kscale(S)
    packed_xT = pack_weight(n((K, T)) * s)
    return {
        "x_words": packed_xT[0],
        "x_scales": packed_xT[1],
        "w1": (n((K, H)) / np.sqrt(K) / s).astype(np.float32),
        "tab": n((H, J)).astype(np.float32),
        "gn": (np.random.uniform(0.5, 1.5, (H, 1)) * u[:, None]).astype(np.float32),
        "w2": (n((H, N)) / np.sqrt(H) / u[:, None]).astype(np.float32),
        "gs": (np.random.uniform(0.5, 1.5, (K, 1)) / s).astype(np.float32),
        "offs": striped(np.random.permutation(T)[:S]),
        "n1": striped8(np.stack([np.random.permutation(S) for _ in range(8)])),
        "n2": striped8(np.stack([np.random.permutation(S) for _ in range(8)])),
        "n3": striped(np.random.randint(0, J, S)),
        "n4": striped(np.random.permutation(S)),
        "cand": striped(np.random.permutation(T)[:C]),
        "n5": striped(np.random.permutation(S)),
        "n6": striped(np.random.permutation(S)),
    }


def reference(x_words, x_scales, w1, tab, gn, w2, gs, offs, n1, n2, n3, n4, cand, n5, n6):
    xq = unpack_weight(x_words, x_scales)[:, unstriped(offs)]
    y = mxq(f64(w1), 0, "e4m3").T @ xq
    ex = np.exp(y)
    z = f64(gn) * (np.log(ex + ex[np.arange(H)[:, None], runs(n1, H)]) - (y[np.arange(H)[:, None], runs(n2, H)]))
    a = mxq(f64(w2), 0, "e4m3").T @ mxq(z, 0, "e4m3")
    x_cand = unpack_weight(x_words, x_scales)[:, unstriped(cand)]
    z2 = f64(gs) * (np.abs(y - y[:, unstriped(n4)] - f64(tab)[:, unstriped(n3)]))
    b = 0.0625 * ((x_cand.T @ mxq(z2, 0, "e4m3")))
    return (a - a[:, unstriped(n5)]) / (np.abs(b) + np.abs(b[:, unstriped(n6)]) + 0.5)

@@ -1,0 +1,261 @@
+from contextlib import ExitStack
+
+import concourse.mybir as mybir
+from concourse.masks import make_identity
+
+F32 = mybir.dt.float32
+BF16 = mybir.dt.bfloat16
+U32 = mybir.dt.uint32
+I32 = mybir.dt.int32
+U16 = mybir.dt.uint16
+U8 = mybir.dt.uint8
+FP8X4 = mybir.dt.float8_e4m3fn_x4
+ALU = mybir.AluOpType
+ACT = mybir.ActivationFunctionType
+
+P = 128
+T = 2048
+S = 512
+HALF = 256
+FLOPS = 3 * 2 * 512 * 512 * 512
+
+
+def tile_picked_fkcdnormblsekindd_none_p_kernel(tc, x_words, x_scales, w1, tab, gn, w2, gs, offs, n1, n2, n3, n4, cand, n5, n6, out):
+    nc = tc.nc
+    with ExitStack() as ctx:
+        keep = ctx.enter_context(tc.tile_pool(name="keep", bufs=1))
+        work = ctx.enter_context(tc.tile_pool(name="work", bufs=3))
+        psum = ctx.enter_context(tc.psum_pool(name="psum", bufs=1))
+
+        def load_list(src, name):
+            lst = keep.tile([P, S // 16], U16, name=name)
+            nc.sync.dma_start(lst[:], src)
+            return lst
+
+        def half(lst, h):
+            return lst[:, h * 16 : (h + 1) * 16]
+
+        def cols(h):
+            return slice(h * HALF, (h + 1) * HALF)
+
+        offs_l = load_list(offs, "offs_l")
+        cand_l = load_list(cand, "cand_l")
+        xs = keep.tile([P, T], U8, name="xs", align_bytes=64)
+        for q in range(4):
+            nc.sync.dma_start(xs[32 * q : 32 * q + 32, :].bitcast(I32), x_scales[0, 4 * q : 4 * q + 4, :].bitcast(I32).partition_broadcast(8))
+        xw = keep.tile([P, T], I32, name="xw", align_bytes=64)
+        nc.sync.dma_start(xw[:], x_words[0].rearrange("p n t -> p (n t)").bitcast(I32))
+        w1_rows = w1.rearrange("(p j) c -> p j c", j=4)
+        w1_raw = []
+        for h in range(2):
+            raw = keep.tile([P, 4, HALF], F32, name="w1_raw%d" % h)
+            nc.sync.dma_start(raw[:], w1_rows[:, :, cols(h)])
+            w1_raw.append(raw)
+        n3_l = load_list(n3, "n3_l")
+        n4_l = load_list(n4, "n4_l")
+        tab_rows = tab.rearrange("(p t) c -> p t c", t=4)
+        tab_t = []
+        for t in range(4):
+            tt = keep.tile([P, S], F32, name="tab%d" % t)
+            nc.sync.dma_start(tt[:], tab_rows[:, t, :])
+            tab_t.append(tt)
+        n1_l = load_list(n1, "n1_l")
+        gs_sb = keep.tile([P, 4], F32, name="gs_sb")
+        nc.sync.dma_start(gs_sb[:], gs.rearrange("(p t) o -> p (t o)", t=4))
+        gn_sb = keep.tile([P, 4], F32, name="gn_sb")
+        nc.sync.dma_start(gn_sb[:], gn.rearrange("(p t) o -> p (t o)", t=4))
+        n2_l = load_list(n2, "n2_l")
+        w2_raw = keep.tile([P, 4, S], F32, name="w2_raw")
+        nc.sync.dma_start(w2_raw[:], w2.rearrange("(p j) c -> p j c", j=4))
+        n6_l = load_list(n6, "n6_l")
+        n5_l = load_list(n5, "n5_l")
+
+        ngn = keep.tile([P, 4], F32, name="ngn")
+        nc.gpsimd.tensor_scalar(ngn[:], gn_sb[:], -1.0, 0.0, ALU.mult, ALU.add)
+
+        def mx_tiles(name):
+            return (keep.tile([P, S], U32, name=name + "_w", align_bytes=64), keep.tile([P, S], U8, name=name + "_s", align_bytes=64))
+
+        xo_w, xo_s = mx_tiles("xo")
+        xc_w, xc_s = mx_tiles("xc")
+        nc.vector.tensor_copy(xo_s[:], xs[:].indirect(offs_l[:]))
+        nc.vector.tensor_copy(xc_s[:], xs[:].indirect(cand_l[:]))
+        nc.vector.tensor_copy(xo_w[:], xw[:].bitcast(U32).indirect(offs_l[:]))
+        nc.vector.tensor_copy(xc_w[:], xw[:].bitcast(U32).indirect(cand_l[:]))
+
+        w1_bf = keep.tile([P, 4 * S], BF16, name="w1_bf", align_bytes=64)
+        w1_view = w1_bf[:].rearrange("p (t m j) -> p m j t", t=4, j=4)
+        nc.scalar.copy(w1_view[:, 0:64], w1_raw[0][:].rearrange("p j (m t) -> p m j t", t=4))
+        nc.vector.tensor_copy(w1_view[:, 64:128], w1_raw[1][:].rearrange("p j (m t) -> p m j t", t=4))
+        w1_w, w1_s = mx_tiles("w1q")
+        for t in range(4):
+            nc.vector.quantize_mx(w1_w[:, t * P : (t + 1) * P].bitcast(FP8X4), w1_s[:, t * P : (t + 1) * P], w1_bf[:, t * S : (t + 1) * S])
+
+        def product(tag, lw, ls, i, rw, rs):
+            acc = psum.tile([P, S], F32, name=tag, tag=tag)
+            c = slice(i * P, (i + 1) * P)
+            nc.tensor.matmul_mx(acc[:], lhsT=lw[:, c].bitcast(FP8X4), lhsT_scale=ls[:, c], rhs=rw[:].bitcast(FP8X4), rhs_scale=rs[:], start=True, stop=True)
+            return acc
+
+        ident = keep.tile([P, P], F32, name="ident")
+        make_identity(nc, ident[:])
+
+        def bank(i):
+            return psum.tile([P, S], F32, name="bank%d" % i, tag="bank%d" % i)
+
+        def blk(b):
+            return slice(b * P, (b + 1) * P)
+
+        def turn(dst, srcs):
+            for i, src in enumerate(srcs):
+                nc.tensor.matmul(dst, lhsT=src, rhs=ident[:], is_transpose=True, start=(i == 0), stop=(i == len(srcs) - 1))
+
+        y_ps = [product("bank%d" % t, w1_w, w1_s, t, xo_w, xo_s) for t in range(4)]
+        y_t = []
+        ex_t = []
+        ex2 = [keep.tile([P, 2, S], F32, name="ex_again%d" % i, tag="ex_again%d" % i, align_bytes=64) for i in range(2)]
+
+        def exp_of(t, tag):
+            e = keep.tile([P, S], F32, name="ex%d" % t, tag=tag)
+            nc.scalar.activation(e[:], y_t[t][:], ACT.Exp)
+            nc.sync.dma_start(ex2[t // 2][:, t % 2, :], e[:])
+            ex_t.append(e)
+
+        for t in range(4):
+            y = keep.tile([P, S], F32, name="y%d" % t)
+            nc.vector.tensor_copy(y[:], y_ps[t][:])
+            y_t.append(y)
+            if t < 2:
+                exp_of(t, "ex%d" % t)
+
+        z2_w, z2_s = mx_tiles("z2q")
+        back = [bank(b) for b in range(4)]
+        for h in range(2):
+            for pair in range(2):
+                ut = bank(4 + 2 * h + pair)
+                for i in range(2):
+                    t = 2 * pair + i
+                    d = keep.tile([P, HALF], F32, name="d%d%d" % (t, h))
+                    nc.vector.tensor_tensor(d[:], tab_t[t][:].indirect(half(n3_l, h)), y_t[t][:, cols(h)], ALU.subtract)
+                    g4 = keep.tile([P, HALF], F32, name="g4", tag="g4_%d%d" % (t, h))
+                    nc.scalar.activation(g4[:], y_t[t][:].indirect(half(n4_l, h)), ACT.Copy)
+                    for b in range(2):
+                        turn(ut[:, blk(2 * i + b)], [d[:, blk(b)], g4[:, blk(b)]])
+                if pair == 0:
+                    abs_h = keep.tile([P, 2, S], F32, name="abs_h%d" % h, tag="abs_h%d" % h)
+                abst = abs_h[:, pair, :]
+                nc.scalar.activation(abst, ut[:], ACT.Abs)
+                for i in range(2):
+                    for b in range(2):
+                        turn(back[2 * h + b][:, blk(2 * pair + i)], [abst[:, blk(2 * i + b)]])
+        exp_of(2, "g4_21")
+        exp_of(3, "g4_31")
+
+        def fetch_ex(t, h):
+            nc.vector.tensor_tensor(ssum[t // 2][:, t % 2, cols(h)], ex_t[t][:].indirect(half(n1_l, h)), ex2[t // 2][:, t % 2, cols(h)], ALU.add)
+
+        z2_bf = keep.tile([P, 4 * S], BF16, name="z2_bf", tag="z2_bf", align_bytes=64)
+        ssum = [keep.tile([P, 2, S], F32, name="ssum0")]
+
+        def scale_z2(b):
+            nc.vector.tensor_tensor(
+                z2_bf[:, b * S : (b + 1) * S].rearrange("p (j t) -> p j t", t=4),
+                back[b][:].rearrange("p (t j) -> p j t", t=4),
+                gs_sb[:].unsqueeze(1).to_broadcast([P, P, 4]),
+                ALU.mult,
+            )
+
+        def quantize_half(w, s, bf, h):
+            nc.vector.quantize_mx(w[:, cols(h)].bitcast(FP8X4), s[:, cols(h)], bf[:, h * 4 * HALF : (h + 1) * 4 * HALF])
+
+        scale_z2(0)
+        scale_z2(1)
+        fetch_ex(0, 0)
+        fetch_ex(0, 1)
+        fetch_ex(1, 0)
+        scale_z2(2)
+        scale_z2(3)
+        fetch_ex(1, 1)
+        nc.vector.quantize_mx(z2_w[:].bitcast(FP8X4), z2_s[:], z2_bf[:])
+        ssum.append(keep.tile([P, 2, S], F32, name="ssum1", tag="z2_bf", align_bytes=64))
+        for t in range(2, 4):
+            for h in range(2):
+                fetch_ex(t, h)
+        lg = [keep.tile([P, 2, S], F32, name="lg0", tag="abs_h1")]
+        nc.scalar.activation(lg[0][:], ssum[0][:], ACT.Ln)
+
+        b_ps = [product("bank%d" % (4 + m), xc_w, xc_s, m, z2_w, z2_s) for m in range(4)]
+
+        w2_bf = keep.tile([P, 4 * S], BF16, name="w2_bf", tag="ex_again1", align_bytes=64)
+        nc.vector.tensor_copy(w2_bf[:].rearrange("p (c i j) -> p c j i", i=4, j=4), w2_raw[:].rearrange("p j (c i) -> p c j i", i=4))
+        w2_w, w2_s = mx_tiles("w2q")
+
+        lnd = keep.tile([P, 4, S], F32, name="lnd", tag="lnd")
+        for m in range(4):
+            c = keep.tile([P, S], F32, name="c%d" % m)
+            nc.scalar.activation(c[:], b_ps[m][:], ACT.Abs, scale=0.0625)
+            g6 = keep.tile([P, S], F32, name="g6", tag="g6_%d" % m)
+            for h in range(2):
+                nc.scalar.activation(g6[:, cols(h)], c[:].indirect(half(n6_l, h)), ACT.Copy)
+            dt = bank(m % 2)
+            for b in range(4):
+                turn(dt[:, blk(b)], [c[:, blk(b)], g6[:, blk(b)]])
+            if m == 1:
+                lg.append(keep.tile([P, 2, S], F32, name="lg1", tag="g6_0"))
+                nc.scalar.activation(lg[1][:], ssum[1][:], ACT.Ln)
+            nc.scalar.activation(lnd[:, m, :], dt[:], ACT.Ln, bias=0.5)
+        rec = keep.tile([P, 4, S], F32, name="rec")
+        nc.scalar.activation(rec[:], lnd[:], ACT.Exp, scale=-1.0)
+
+        zf = keep.tile([P, 4, S], F32, name="zf")
+        z_w, z_s = mx_tiles("zq")
+        z_bf = keep.tile([P, 4 * S], BF16, name="z_bf", align_bytes=64)
+
+        def fetch_y(t, h):
+            nc.vector.tensor_tensor(zf[:, t, cols(h)], y_t[t][:].indirect(half(n2_l, h)), lg[t // 2][:, t % 2, cols(h)], ALU.subtract)
+
+        def scale_z(h):
+            nc.vector.tensor_tensor(
+                z_bf[:, h * 4 * HALF : (h + 1) * 4 * HALF].rearrange("p (c i t) -> p c t i", i=4, t=4),
+                zf[:, :, cols(h)].rearrange("p t (c i) -> p c t i", i=4),
+                ngn[:].unsqueeze(1).unsqueeze(3).to_broadcast([P, HALF // 4, 4, 4]),
+                ALU.mult,
+            )
+
+        fetch_y(0, 0)
+        nc.vector.quantize_mx(w2_w[:].bitcast(FP8X4), w2_s[:], w2_bf[:])
+        fetch_y(1, 0)
+        fetch_y(0, 1)
+        fetch_y(1, 1)
+        fetch_y(2, 0)
+        fetch_y(3, 0)
+        fetch_y(2, 1)
+        scale_z(0)
+        fetch_y(3, 1)
+        quantize_half(z_w, z_s, z_bf, 0)
+        scale_z(1)
+        quantize_half(z_w, z_s, z_bf, 1)
+
+        a_ps = [product("bank%d" % (4 + m), w2_w, w2_s, m, z_w, z_s) for m in range(4)]
+        late = keep.tile([P, 4, S], F32, name="late", tag="lnd")
+        for m in range(4):
+            a = keep.tile([P, S], F32, name="a%d" % m)
+            if m < 2:
+                g5 = keep.tile([P, S], F32, name="g5_%d" % m)[:]
+                nc.vector.tensor_copy(a[:], a_ps[m][:])
+            else:
+                g5 = late[:, m, :]
+                nc.scalar.copy(a[:], a_ps[m][:])
+            for h in range(2):
+                if m < 2:
+                    nc.vector.tensor_copy(g5[:, cols(h)], a[:].indirect(half(n5_l, h)))
+                else:
+                    nc.scalar.activation(g5[:, cols(h)], a[:].indirect(half(n5_l, h)), ACT.Copy)
+            num = keep.tile([P, S], F32, name="num%d" % m)
+            nc.vector.tensor_tensor(num[:], a_ps[m][:], g5, ALU.subtract)
+            rb = bank(m)
+            for b in range(4):
+                turn(rb[:, blk(b)], [rec[:, m, blk(b)]])
+            res = work.tile([P, S], F32, name="res", bufs=4)
+            nc.vector.tensor_tensor(res[:], rb[:], num[:], ALU.mult)
+            nc.sync.dma_start(out[m * P : (m + 1) * P, :], res[:])

@@ -46,10 +46,11 @@ def tile_picked_fkcdnormblsekindd_none_p_kernel(tc, x_words, x_scales, w1, tab, 
         xw = keep.tile([P, T], I32, name="xw", align_bytes=64)
         nc.sync.dma_start(xw[:], x_words[0].rearrange("p n t -> p (n t)").bitcast(I32))
         w1_rows = w1.rearrange("(p j) c -> p j c", j=4)
+        w1_cuts = (0, 256, 384, 512)
         w1_raw = []
-        for h in range(2):
-            raw = keep.tile([P, 4, HALF], F32, name="w1_raw%d" % h)
-            nc.sync.dma_start(raw[:], w1_rows[:, :, cols(h)])
+        for i in range(3):
+            raw = keep.tile([P, 4, w1_cuts[i + 1] - w1_cuts[i]], F32, name="w1_raw%d" % i)
+            nc.sync.dma_start(raw[:], w1_rows[:, :, w1_cuts[i] : w1_cuts[i + 1]])
             w1_raw.append(raw)
         n3_l = load_list(n3, "n3_l")
         n4_l = load_list(n4, "n4_l")
@@ -77,19 +78,21 @@ def tile_picked_fkcdnormblsekindd_none_p_kernel(tc, x_words, x_scales, w1, tab, 
             return (keep.tile([P, S], U32, name=name + "_w", align_bytes=64), keep.tile([P, S], U8, name=name + "_s", align_bytes=64))
 
         xo_w, xo_s = mx_tiles("xo")
-        xc_w, xc_s = mx_tiles("xc")
+        xc_s = keep.tile([P, S], U8, name="xc_s", align_bytes=64)
         nc.vector.tensor_copy(xo_s[:], xs[:].indirect(offs_l[:]))
         nc.vector.tensor_copy(xc_s[:], xs[:].indirect(cand_l[:]))
         nc.vector.tensor_copy(xo_w[:], xw[:].bitcast(U32).indirect(offs_l[:]))
-        nc.vector.tensor_copy(xc_w[:], xw[:].bitcast(U32).indirect(cand_l[:]))
 
-        w1_bf = keep.tile([P, 4 * S], BF16, name="w1_bf", align_bytes=64)
+        w1_bf = keep.tile([P, 4 * S], BF16, name="w1_bf", tag="w1_bf", align_bytes=64)
         w1_view = w1_bf[:].rearrange("p (t m j) -> p m j t", t=4, j=4)
         nc.scalar.copy(w1_view[:, 0:64], w1_raw[0][:].rearrange("p j (m t) -> p m j t", t=4))
-        nc.vector.tensor_copy(w1_view[:, 64:128], w1_raw[1][:].rearrange("p j (m t) -> p m j t", t=4))
+        for i in range(1, 3):
+            nc.vector.tensor_copy(w1_view[:, w1_cuts[i] // 4 : w1_cuts[i + 1] // 4], w1_raw[i][:].rearrange("p j (m t) -> p m j t", t=4))
         w1_w, w1_s = mx_tiles("w1q")
         for t in range(4):
             nc.vector.quantize_mx(w1_w[:, t * P : (t + 1) * P].bitcast(FP8X4), w1_s[:, t * P : (t + 1) * P], w1_bf[:, t * S : (t + 1) * S])
+        xc_w = keep.tile([P, S], U32, name="xc_w", tag="w1_bf", align_bytes=64)
+        nc.vector.tensor_copy(xc_w[:], xw[:].bitcast(U32).indirect(cand_l[:]))
 
         def product(tag, lw, ls, i, rw, rs):
             acc = psum.tile([P, S], F32, name=tag, tag=tag)
@@ -123,33 +126,48 @@ def tile_picked_fkcdnormblsekindd_none_p_kernel(tc, x_words, x_scales, w1, tab, 
 
         for t in range(4):
             y = keep.tile([P, S], F32, name="y%d" % t)
-            nc.vector.tensor_copy(y[:], y_ps[t][:])
+            nc.scalar.copy(y[:], y_ps[t][:])
             y_t.append(y)
-            if t < 2:
-                exp_of(t, "ex%d" % t)
+
+        def tab_less_y(t, h):
+            d = keep.tile([P, HALF], F32, name="d%d%d" % (t, h))
+            nc.vector.tensor_tensor(d[:], tab_t[t][:].indirect(half(n3_l, h)), y_t[t][:, cols(h)], ALU.subtract)
+            return d
 
         z2_w, z2_s = mx_tiles("z2q")
-        back = [bank(b) for b in range(4)]
-        for h in range(2):
-            for pair in range(2):
-                ut = bank(4 + 2 * h + pair)
-                for i in range(2):
-                    t = 2 * pair + i
-                    d = keep.tile([P, HALF], F32, name="d%d%d" % (t, h))
-                    nc.vector.tensor_tensor(d[:], tab_t[t][:].indirect(half(n3_l, h)), y_t[t][:, cols(h)], ALU.subtract)
-                    g4 = keep.tile([P, HALF], F32, name="g4", tag="g4_%d%d" % (t, h))
-                    nc.scalar.activation(g4[:], y_t[t][:].indirect(half(n4_l, h)), ACT.Copy)
-                    for b in range(2):
-                        turn(ut[:, blk(2 * i + b)], [d[:, blk(b)], g4[:, blk(b)]])
-                if pair == 0:
-                    abs_h = keep.tile([P, 2, S], F32, name="abs_h%d" % h, tag="abs_h%d" % h)
-                abst = abs_h[:, pair, :]
-                nc.scalar.activation(abst, ut[:], ACT.Abs)
-                for i in range(2):
-                    for b in range(2):
-                        turn(back[2 * h + b][:, blk(2 * pair + i)], [abst[:, blk(2 * i + b)]])
-        exp_of(2, "g4_21")
-        exp_of(3, "g4_31")
+        ut = [bank(4), bank(5)]
+        for t in range(4):
+            d = tab_less_y(t, 0)
+            g4 = keep.tile([P, HALF], F32, name="g4_%d" % t)
+            nc.scalar.activation(g4[:], y_t[t][:].indirect(half(n4_l, 0)), ACT.Copy)
+            for b in range(2):
+                turn(ut[t // 2][:, blk(2 * (t % 2) + b)], [d[:, blk(b)], g4[:, blk(b)]])
+        exp_of(0, "ex0")
+        exp_of(1, "ex1")
+        back = [bank(0), bank(1)]
+        for pair in range(2):
+            abst = keep.tile([P, S], F32, name="abst%d" % pair)
+            nc.scalar.activation(abst[:], ut[pair][:], ACT.Abs)
+            for i in range(2):
+                for b in range(2):
+                    turn(back[b][:, blk(2 * pair + i)], [abst[:, blk(2 * i + b)]])
+        u1 = keep.tile([P, 4, HALF], F32, name="u1")
+        absu = keep.tile([P, 4, HALF], F32, name="absu")
+        for pair in range(2):
+            ds = [tab_less_y(2 * pair + i, 1) for i in range(2)]
+            for i in range(2):
+                t = 2 * pair + i
+                nc.vector.tensor_tensor(u1[:, t, :], y_t[t][:].indirect(half(n4_l, 1)), ds[i][:], ALU.add)
+            nc.scalar.activation(absu[:, 2 * pair : 2 * pair + 2, :], u1[:, 2 * pair : 2 * pair + 2, :], ACT.Abs)
+            exp_of(2 + pair, "ex%d" % (2 + pair))
+
+        def weave(dst, src, gain):
+            nc.vector.tensor_tensor(
+                dst.rearrange("p (c i t) -> p c t i", i=4, t=4),
+                src.rearrange("p t (c i) -> p c t i", i=4),
+                gain[:].unsqueeze(1).unsqueeze(3).to_broadcast([P, HALF // 4, 4, 4]),
+                ALU.mult,
+            )
 
         def fetch_ex(t, h):
             nc.vector.tensor_tensor(ssum[t // 2][:, t % 2, cols(h)], ex_t[t][:].indirect(half(n1_l, h)), ex2[t // 2][:, t % 2, cols(h)], ALU.add)
@@ -170,19 +188,21 @@ def tile_picked_fkcdnormblsekindd_none_p_kernel(tc, x_words, x_scales, w1, tab, 
 
         scale_z2(0)
         scale_z2(1)
-        fetch_ex(0, 0)
-        fetch_ex(0, 1)
-        fetch_ex(1, 0)
-        scale_z2(2)
-        scale_z2(3)
-        fetch_ex(1, 1)
+        for t in range(2):
+            for h in range(2):
+                fetch_ex(t, h)
+        weave(z2_bf[:, 4 * HALF :], absu[:], gs_sb)
         nc.vector.quantize_mx(z2_w[:].bitcast(FP8X4), z2_s[:], z2_bf[:])
         ssum.append(keep.tile([P, 2, S], F32, name="ssum1", tag="z2_bf", align_bytes=64))
         for t in range(2, 4):
             for h in range(2):
                 fetch_ex(t, h)
-        lg = [keep.tile([P, 2, S], F32, name="lg0", tag="abs_h1")]
-        nc.scalar.activation(lg[0][:], ssum[0][:], ACT.Ln)
+        lg = [keep.tile([P, 2, S], F32, name="lg%d" % i) for i in range(2)]
+
+        def log_of(t):
+            nc.scalar.activation(lg[t // 2][:, t % 2, :], ssum[t // 2][:, t % 2, :], ACT.Ln)
+
+        log_of(0)
 
         b_ps = [product("bank%d" % (4 + m), xc_w, xc_s, m, z2_w, z2_s) for m in range(4)]
 
@@ -190,22 +210,29 @@ def tile_picked_fkcdnormblsekindd_none_p_kernel(tc, x_words, x_scales, w1, tab, 
         nc.vector.tensor_copy(w2_bf[:].rearrange("p (c i j) -> p c j i", i=4, j=4), w2_raw[:].rearrange("p j (c i) -> p c j i", i=4))
         w2_w, w2_s = mx_tiles("w2q")
 
-        lnd = keep.tile([P, 4, S], F32, name="lnd", tag="lnd")
+        lnd = [keep.tile([P, 2, S], F32, name="lnd%d" % i, tag="lnd%d" % i) for i in range(2)]
+        den = []
+
+        def log_den(m):
+            nc.scalar.activation(lnd[m // 2][:, m % 2, :], den[m][:], ACT.Ln, bias=0.5)
+
         for m in range(4):
             c = keep.tile([P, S], F32, name="c%d" % m)
             nc.scalar.activation(c[:], b_ps[m][:], ACT.Abs, scale=0.0625)
             g6 = keep.tile([P, S], F32, name="g6", tag="g6_%d" % m)
             for h in range(2):
                 nc.scalar.activation(g6[:, cols(h)], c[:].indirect(half(n6_l, h)), ACT.Copy)
-            dt = bank(m % 2)
+            den.append(bank(m))
             for b in range(4):
-                turn(dt[:, blk(b)], [c[:, blk(b)], g6[:, blk(b)]])
-            if m == 1:
-                lg.append(keep.tile([P, 2, S], F32, name="lg1", tag="g6_0"))
-                nc.scalar.activation(lg[1][:], ssum[1][:], ACT.Ln)
-            nc.scalar.activation(lnd[:, m, :], dt[:], ACT.Ln, bias=0.5)
-        rec = keep.tile([P, 4, S], F32, name="rec")
-        nc.scalar.activation(rec[:], lnd[:], ACT.Exp, scale=-1.0)
+                turn(den[m][:, blk(b)], [c[:, blk(b)], g6[:, blk(b)]])
+            if m < 3:
+                log_of(m + 1)
+            if m > 0:
+                log_den(m - 1)
+        log_den(3)
+        rec = [keep.tile([P, 2, S], F32, name="rec0", tag="g6_3"), keep.tile([P, 2, S], F32, name="rec1")]
+        for i in range(2):
+            nc.scalar.activation(rec[i][:], lnd[i][:], ACT.Exp, scale=-1.0)
 
         zf = keep.tile([P, 4, S], F32, name="zf")
         z_w, z_s = mx_tiles("zq")
@@ -215,17 +242,12 @@ def tile_picked_fkcdnormblsekindd_none_p_kernel(tc, x_words, x_scales, w1, tab, 
             nc.vector.tensor_tensor(zf[:, t, cols(h)], y_t[t][:].indirect(half(n2_l, h)), lg[t // 2][:, t % 2, cols(h)], ALU.subtract)
 
         def scale_z(h):
-            nc.vector.tensor_tensor(
-                z_bf[:, h * 4 * HALF : (h + 1) * 4 * HALF].rearrange("p (c i t) -> p c t i", i=4, t=4),
-                zf[:, :, cols(h)].rearrange("p t (c i) -> p c t i", i=4),
-                ngn[:].unsqueeze(1).unsqueeze(3).to_broadcast([P, HALF // 4, 4, 4]),
-                ALU.mult,
-            )
+            weave(z_bf[:, h * 4 * HALF : (h + 1) * 4 * HALF], zf[:, :, cols(h)], ngn)
 
         fetch_y(0, 0)
         nc.vector.quantize_mx(w2_w[:].bitcast(FP8X4), w2_s[:], w2_bf[:])
-        fetch_y(1, 0)
         fetch_y(0, 1)
+        fetch_y(1, 0)
         fetch_y(1, 1)
         fetch_y(2, 0)
         fetch_y(3, 0)
@@ -237,14 +259,14 @@ def tile_picked_fkcdnormblsekindd_none_p_kernel(tc, x_words, x_scales, w1, tab, 
         quantize_half(z_w, z_s, z_bf, 1)
 
         a_ps = [product("bank%d" % (4 + m), w2_w, w2_s, m, z_w, z_s) for m in range(4)]
-        late = keep.tile([P, 4, S], F32, name="late", tag="lnd")
+        late = keep.tile([P, 2, S], F32, name="late", tag="lnd1")
         for m in range(4):
-            a = keep.tile([P, S], F32, name="a%d" % m)
+            a = keep.tile([P, S], F32, name="a%d" % m, tag=("lnd0" if m == 2 else "a%d" % m))
             if m < 2:
                 g5 = keep.tile([P, S], F32, name="g5_%d" % m)[:]
                 nc.vector.tensor_copy(a[:], a_ps[m][:])
             else:
-                g5 = late[:, m, :]
+                g5 = late[:, m - 2, :]
                 nc.scalar.copy(a[:], a_ps[m][:])
             for h in range(2):
                 if m < 2:
@@ -255,7 +277,13 @@ def tile_picked_fkcdnormblsekindd_none_p_kernel(tc, x_words, x_scales, w1, tab, 
             nc.vector.tensor_tensor(num[:], a_ps[m][:], g5, ALU.subtract)
             rb = bank(m)
             for b in range(4):
-                turn(rb[:, blk(b)], [rec[:, m, blk(b)]])
+                turn(rb[:, blk(b)], [rec[m // 2][:, m % 2, blk(b)]])
             res = work.tile([P, S], F32, name="res", bufs=4)
-            nc.vector.tensor_tensor(res[:], rb[:], num[:], ALU.mult)
-            nc.sync.dma_start(out[m * P : (m + 1) * P, :], res[:])
+            if m < 3:
+                nc.vector.tensor_tensor(res[:], rb[:], num[:], ALU.mult)
+                nc.sync.dma_start(out[m * P : (m + 1) * P, :], res[:])
+            else:
+                for h in range(2):
+                    nc.vector.tensor_tensor(res[:, cols(h)], rb[:, cols(h)], num[:, cols(h)], ALU.mult)
+                    queue = nc.sync if h == 0 else nc.scalar
+                    queue.dma_start(out[m * P : (m + 1) * P, cols(h)], res[:, cols(h)])

@@ -46,11 +46,10 @@ def tile_picked_fkcdnormblsekindd_none_p_kernel(tc, x_words, x_scales, w1, tab, 
         xw = keep.tile([P, T], I32, name="xw", align_bytes=64)
         nc.sync.dma_start(xw[:], x_words[0].rearrange("p n t -> p (n t)").bitcast(I32))
         w1_rows = w1.rearrange("(p j) c -> p j c", j=4)
-        w1_cuts = (0, 256, 384, 512)
         w1_raw = []
-        for i in range(3):
-            raw = keep.tile([P, 4, w1_cuts[i + 1] - w1_cuts[i]], F32, name="w1_raw%d" % i)
-            nc.sync.dma_start(raw[:], w1_rows[:, :, w1_cuts[i] : w1_cuts[i + 1]])
+        for i in range(2):
+            raw = keep.tile([P, 2, S], F32, name="w1_raw%d" % i)
+            nc.sync.dma_start(raw[:], w1_rows[:, 2 * i : 2 * i + 2, :])
             w1_raw.append(raw)
         n3_l = load_list(n3, "n3_l")
         n4_l = load_list(n4, "n4_l")
@@ -72,7 +71,7 @@ def tile_picked_fkcdnormblsekindd_none_p_kernel(tc, x_words, x_scales, w1, tab, 
         n5_l = load_list(n5, "n5_l")
 
         ngn = keep.tile([P, 4], F32, name="ngn")
-        nc.gpsimd.tensor_scalar(ngn[:], gn_sb[:], -1.0, 0.0, ALU.mult, ALU.add)
+        nc.vector.tensor_scalar(ngn[:], gn_sb[:], -1.0, 0.0, ALU.mult, ALU.add)
 
         def mx_tiles(name):
             return (keep.tile([P, S], U32, name=name + "_w", align_bytes=64), keep.tile([P, S], U8, name=name + "_s", align_bytes=64))
@@ -85,9 +84,8 @@ def tile_picked_fkcdnormblsekindd_none_p_kernel(tc, x_words, x_scales, w1, tab, 
 
         w1_bf = keep.tile([P, 4 * S], BF16, name="w1_bf", tag="w1_bf", align_bytes=64)
         w1_view = w1_bf[:].rearrange("p (t m j) -> p m j t", t=4, j=4)
-        nc.scalar.copy(w1_view[:, 0:64], w1_raw[0][:].rearrange("p j (m t) -> p m j t", t=4))
-        for i in range(1, 3):
-            nc.vector.tensor_copy(w1_view[:, w1_cuts[i] // 4 : w1_cuts[i + 1] // 4], w1_raw[i][:].rearrange("p j (m t) -> p m j t", t=4))
+        nc.scalar.copy(w1_view[:, :, 0:2, :], w1_raw[0][:].rearrange("p j (m t) -> p m j t", t=4))
+        nc.vector.tensor_copy(w1_view[:, :, 2:4, :], w1_raw[1][:].rearrange("p j (m t) -> p m j t", t=4))
         w1_w, w1_s = mx_tiles("w1q")
         for t in range(4):
             nc.vector.quantize_mx(w1_w[:, t * P : (t + 1) * P].bitcast(FP8X4), w1_s[:, t * P : (t + 1) * P], w1_bf[:, t * S : (t + 1) * S])
@@ -152,7 +150,7 @@ def tile_picked_fkcdnormblsekindd_none_p_kernel(tc, x_words, x_scales, w1, tab, 
                 for b in range(2):
                     turn(back[b][:, blk(2 * pair + i)], [abst[:, blk(2 * i + b)]])
         u1 = keep.tile([P, 4, HALF], F32, name="u1")
-        absu = keep.tile([P, 4, HALF], F32, name="absu")
+        absu = keep.tile([P, 4, HALF], F32, name="absu", tag="absu")
         for pair in range(2):
             ds = [tab_less_y(2 * pair + i, 1) for i in range(2)]
             for i in range(2):
@@ -170,10 +168,10 @@ def tile_picked_fkcdnormblsekindd_none_p_kernel(tc, x_words, x_scales, w1, tab, 
             )
 
         def fetch_ex(t, h):
-            nc.vector.tensor_tensor(ssum[t // 2][:, t % 2, cols(h)], ex_t[t][:].indirect(half(n1_l, h)), ex2[t // 2][:, t % 2, cols(h)], ALU.add)
+            nc.vector.tensor_tensor(ssum[t][:, cols(h)], ex_t[t][:].indirect(half(n1_l, h)), ex2[t // 2][:, t % 2, cols(h)], ALU.add)
 
         z2_bf = keep.tile([P, 4 * S], BF16, name="z2_bf", tag="z2_bf", align_bytes=64)
-        ssum = [keep.tile([P, 2, S], F32, name="ssum0")]
+        ssum = [keep.tile([P, S], F32, name="ssum0")[:]]
 
         def scale_z2(b):
             nc.vector.tensor_tensor(
@@ -188,19 +186,20 @@ def tile_picked_fkcdnormblsekindd_none_p_kernel(tc, x_words, x_scales, w1, tab, 
 
         scale_z2(0)
         scale_z2(1)
-        for t in range(2):
-            for h in range(2):
-                fetch_ex(t, h)
+        for h in range(2):
+            fetch_ex(0, h)
         weave(z2_bf[:, 4 * HALF :], absu[:], gs_sb)
         nc.vector.quantize_mx(z2_w[:].bitcast(FP8X4), z2_s[:], z2_bf[:])
-        ssum.append(keep.tile([P, 2, S], F32, name="ssum1", tag="z2_bf", align_bytes=64))
-        for t in range(2, 4):
+        ssum.append(keep.tile([P, S], F32, name="ssum1", tag="absu")[:])
+        ssum23 = keep.tile([P, 2, S], F32, name="ssum23", tag="z2_bf", align_bytes=64)
+        ssum.extend([ssum23[:, 0, :], ssum23[:, 1, :]])
+        for t in range(1, 4):
             for h in range(2):
                 fetch_ex(t, h)
         lg = [keep.tile([P, 2, S], F32, name="lg%d" % i) for i in range(2)]
 
         def log_of(t):
-            nc.scalar.activation(lg[t // 2][:, t % 2, :], ssum[t // 2][:, t % 2, :], ACT.Ln)
+            nc.scalar.activation(lg[t // 2][:, t % 2, :], ssum[t], ACT.Ln)
 
         log_of(0)
 
@@ -219,14 +218,16 @@ def tile_picked_fkcdnormblsekindd_none_p_kernel(tc, x_words, x_scales, w1, tab, 
         for m in range(4):
             c = keep.tile([P, S], F32, name="c%d" % m)
             nc.scalar.activation(c[:], b_ps[m][:], ACT.Abs, scale=0.0625)
+            if m < 2:
+                log_of(2 * m + 1)
             g6 = keep.tile([P, S], F32, name="g6", tag="g6_%d" % m)
             for h in range(2):
                 nc.scalar.activation(g6[:, cols(h)], c[:].indirect(half(n6_l, h)), ACT.Copy)
             den.append(bank(m))
             for b in range(4):
                 turn(den[m][:, blk(b)], [c[:, blk(b)], g6[:, blk(b)]])
-            if m < 3:
-                log_of(m + 1)
+            if m == 0:
+                log_of(2)
             if m > 0:
                 log_den(m - 1)
         log_den(3)
@@ -259,22 +260,30 @@ def tile_picked_fkcdnormblsekindd_none_p_kernel(tc, x_words, x_scales, w1, tab, 
         quantize_half(z_w, z_s, z_bf, 1)
 
         a_ps = [product("bank%d" % (4 + m), w2_w, w2_s, m, z_w, z_s) for m in range(4)]
+        a_t = []
+        for m in range(4):
+            a = keep.tile([P, S], F32, name="a%d" % m, tag=("lnd0" if m == 3 else "a%d" % m))
+            if m < 3:
+                nc.vector.tensor_copy(a[:], a_ps[m][:])
+            a_t.append(a)
         late = keep.tile([P, 2, S], F32, name="late", tag="lnd1")
         for m in range(4):
-            a = keep.tile([P, S], F32, name="a%d" % m, tag=("lnd0" if m == 2 else "a%d" % m))
-            if m < 2:
-                g5 = keep.tile([P, S], F32, name="g5_%d" % m)[:]
-                nc.vector.tensor_copy(a[:], a_ps[m][:])
+            if m in (1, 2):
+                g5 = late[:, m - 1, :]
             else:
-                g5 = late[:, m - 2, :]
-                nc.scalar.copy(a[:], a_ps[m][:])
+                g5 = keep.tile([P, S], F32, name="g5_%d" % m)[:]
+            if m == 3:
+                nc.scalar.copy(a_t[m][:], a_ps[m][:])
             for h in range(2):
-                if m < 2:
-                    nc.vector.tensor_copy(g5[:, cols(h)], a[:].indirect(half(n5_l, h)))
+                if m == 0:
+                    nc.vector.tensor_copy(g5[:, cols(h)], a_t[m][:].indirect(half(n5_l, h)))
                 else:
-                    nc.scalar.activation(g5[:, cols(h)], a[:].indirect(half(n5_l, h)), ACT.Copy)
+                    nc.scalar.activation(g5[:, cols(h)], a_t[m][:].indirect(half(n5_l, h)), ACT.Copy)
             num = keep.tile([P, S], F32, name="num%d" % m)
-            nc.vector.tensor_tensor(num[:], a_ps[m][:], g5, ALU.subtract)
+            if m < 3:
+                nc.gpsimd.tensor_tensor(num[:], a_t[m][:], g5, ALU.subtract)
+            else:
+                nc.vector.tensor_tensor(num[:], a_ps[m][:], g5, ALU.subtract)
             rb = bank(m)
             for b in range(4):
                 turn(rb[:, blk(b)], [rec[m // 2][:, m % 2, blk(b)]])

from contextlib import ExitStack

import concourse.mybir as mybir
from concourse.masks import make_identity

F32 = mybir.dt.float32
BF16 = mybir.dt.bfloat16
U32 = mybir.dt.uint32
I32 = mybir.dt.int32
U16 = mybir.dt.uint16
U8 = mybir.dt.uint8
FP8X4 = mybir.dt.float8_e4m3fn_x4
ALU = mybir.AluOpType
ACT = mybir.ActivationFunctionType

P = 128
T = 2048
S = 512
HALF = 256
FLOPS = 3 * 2 * 512 * 512 * 512


def tile_picked_fkcdnormblsekindd_none_p_kernel(tc, x_words, x_scales, w1, tab, gn, w2, gs, offs, n1, n2, n3, n4, cand, n5, n6, out):
    nc = tc.nc
    with ExitStack() as ctx:
        keep = ctx.enter_context(tc.tile_pool(name="keep", bufs=1))
        work = ctx.enter_context(tc.tile_pool(name="work", bufs=3))
        psum = ctx.enter_context(tc.psum_pool(name="psum", bufs=1))

        def load_list(src, name):
            lst = keep.tile([P, S // 16], U16, name=name)
            nc.sync.dma_start(lst[:], src)
            return lst

        def half(lst, h):
            return lst[:, h * 16 : (h + 1) * 16]

        def cols(h):
            return slice(h * HALF, (h + 1) * HALF)

        offs_l = load_list(offs, "offs_l")
        cand_l = load_list(cand, "cand_l")
        xs = keep.tile([P, T], U8, name="xs", align_bytes=64)
        for q in range(4):
            nc.sync.dma_start(xs[32 * q : 32 * q + 32, :].bitcast(I32), x_scales[0, 4 * q : 4 * q + 4, :].bitcast(I32).partition_broadcast(8))
        xw = keep.tile([P, T], I32, name="xw", align_bytes=64)
        nc.sync.dma_start(xw[:], x_words[0].rearrange("p n t -> p (n t)").bitcast(I32))
        w1_rows = w1.rearrange("(p j) c -> p j c", j=4)
        w1_raw = []
        for i in range(2):
            raw = keep.tile([P, 2, S], F32, name="w1_raw%d" % i)
            nc.sync.dma_start(raw[:], w1_rows[:, 2 * i : 2 * i + 2, :])
            w1_raw.append(raw)
        n3_l = load_list(n3, "n3_l")
        n4_l = load_list(n4, "n4_l")
        tab_rows = tab.rearrange("(p t) c -> p t c", t=4)
        tab_t = []
        for t in range(4):
            tt = keep.tile([P, S], F32, name="tab%d" % t)
            nc.sync.dma_start(tt[:], tab_rows[:, t, :])
            tab_t.append(tt)
        n1_l = load_list(n1, "n1_l")
        gs_sb = keep.tile([P, 4], F32, name="gs_sb")
        nc.sync.dma_start(gs_sb[:], gs.rearrange("(p t) o -> p (t o)", t=4))
        gn_sb = keep.tile([P, 4], F32, name="gn_sb")
        nc.sync.dma_start(gn_sb[:], gn.rearrange("(p t) o -> p (t o)", t=4))
        n2_l = load_list(n2, "n2_l")
        w2_raw = keep.tile([P, 4, S], F32, name="w2_raw")
        nc.sync.dma_start(w2_raw[:], w2.rearrange("(p j) c -> p j c", j=4))
        n6_l = load_list(n6, "n6_l")
        n5_l = load_list(n5, "n5_l")

        ngn = keep.tile([P, 4], F32, name="ngn")
        nc.vector.tensor_scalar(ngn[:], gn_sb[:], -1.0, 0.0, ALU.mult, ALU.add)

        def mx_tiles(name):
            return (keep.tile([P, S], U32, name=name + "_w", align_bytes=64), keep.tile([P, S], U8, name=name + "_s", align_bytes=64))

        xo_w, xo_s = mx_tiles("xo")
        xc_s = keep.tile([P, S], U8, name="xc_s", align_bytes=64)
        nc.vector.tensor_copy(xo_s[:], xs[:].indirect(offs_l[:]))
        nc.vector.tensor_copy(xc_s[:], xs[:].indirect(cand_l[:]))
        nc.vector.tensor_copy(xo_w[:], xw[:].bitcast(U32).indirect(offs_l[:]))

        w1_bf = keep.tile([P, 4 * S], BF16, name="w1_bf", tag="w1_bf", align_bytes=64)
        w1_view = w1_bf[:].rearrange("p (t m j) -> p m j t", t=4, j=4)
        nc.scalar.copy(w1_view[:, :, 0:2, :], w1_raw[0][:].rearrange("p j (m t) -> p m j t", t=4))
        nc.vector.tensor_copy(w1_view[:, :, 2:4, :], w1_raw[1][:].rearrange("p j (m t) -> p m j t", t=4))
        w1_w, w1_s = mx_tiles("w1q")
        for t in range(4):
            nc.vector.quantize_mx(w1_w[:, t * P : (t + 1) * P].bitcast(FP8X4), w1_s[:, t * P : (t + 1) * P], w1_bf[:, t * S : (t + 1) * S])
        xc_w = keep.tile([P, S], U32, name="xc_w", tag="w1_bf", align_bytes=64)
        nc.vector.tensor_copy(xc_w[:], xw[:].bitcast(U32).indirect(cand_l[:]))

        def product(tag, lw, ls, i, rw, rs):
            acc = psum.tile([P, S], F32, name=tag, tag=tag)
            c = slice(i * P, (i + 1) * P)
            nc.tensor.matmul_mx(acc[:], lhsT=lw[:, c].bitcast(FP8X4), lhsT_scale=ls[:, c], rhs=rw[:].bitcast(FP8X4), rhs_scale=rs[:], start=True, stop=True)
            return acc

        ident = keep.tile([P, P], F32, name="ident")
        make_identity(nc, ident[:])

        def bank(i):
            return psum.tile([P, S], F32, name="bank%d" % i, tag="bank%d" % i)

        def blk(b):
            return slice(b * P, (b + 1) * P)

        def turn(dst, srcs):
            for i, src in enumerate(srcs):
                nc.tensor.matmul(dst, lhsT=src, rhs=ident[:], is_transpose=True, start=(i == 0), stop=(i == len(srcs) - 1))

        y_ps = [product("bank%d" % t, w1_w, w1_s, t, xo_w, xo_s) for t in range(4)]
        y_t = []
        ex_t = []
        ex2 = [keep.tile([P, 2, S], F32, name="ex_again%d" % i, tag="ex_again%d" % i, align_bytes=64) for i in range(2)]

        def exp_of(t, tag):
            e = keep.tile([P, S], F32, name="ex%d" % t, tag=tag)
            nc.scalar.activation(e[:], y_t[t][:], ACT.Exp)
            nc.sync.dma_start(ex2[t // 2][:, t % 2, :], e[:])
            ex_t.append(e)

        for t in range(4):
            y = keep.tile([P, S], F32, name="y%d" % t)
            nc.scalar.copy(y[:], y_ps[t][:])
            y_t.append(y)

        def tab_less_y(t, h):
            d = keep.tile([P, HALF], F32, name="d%d%d" % (t, h))
            nc.vector.tensor_tensor(d[:], tab_t[t][:].indirect(half(n3_l, h)), y_t[t][:, cols(h)], ALU.subtract)
            return d

        z2_w, z2_s = mx_tiles("z2q")
        ut = [bank(4), bank(5)]
        for t in range(4):
            d = tab_less_y(t, 0)
            g4 = keep.tile([P, HALF], F32, name="g4_%d" % t)
            nc.scalar.activation(g4[:], y_t[t][:].indirect(half(n4_l, 0)), ACT.Copy)
            for b in range(2):
                turn(ut[t // 2][:, blk(2 * (t % 2) + b)], [d[:, blk(b)], g4[:, blk(b)]])
        exp_of(0, "ex0")
        exp_of(1, "ex1")
        back = [bank(0), bank(1)]
        for pair in range(2):
            abst = keep.tile([P, S], F32, name="abst%d" % pair)
            nc.scalar.activation(abst[:], ut[pair][:], ACT.Abs)
            for i in range(2):
                for b in range(2):
                    turn(back[b][:, blk(2 * pair + i)], [abst[:, blk(2 * i + b)]])
        u1 = keep.tile([P, 4, HALF], F32, name="u1")
        absu = keep.tile([P, 4, HALF], F32, name="absu", tag="absu")
        for pair in range(2):
            ds = [tab_less_y(2 * pair + i, 1) for i in range(2)]
            for i in range(2):
                t = 2 * pair + i
                nc.vector.tensor_tensor(u1[:, t, :], y_t[t][:].indirect(half(n4_l, 1)), ds[i][:], ALU.add)
            nc.scalar.activation(absu[:, 2 * pair : 2 * pair + 2, :], u1[:, 2 * pair : 2 * pair + 2, :], ACT.Abs)
            exp_of(2 + pair, "ex%d" % (2 + pair))

        def weave(dst, src, gain):
            nc.vector.tensor_tensor(
                dst.rearrange("p (c i t) -> p c t i", i=4, t=4),
                src.rearrange("p t (c i) -> p c t i", i=4),
                gain[:].unsqueeze(1).unsqueeze(3).to_broadcast([P, HALF // 4, 4, 4]),
                ALU.mult,
            )

        def fetch_ex(t, h):
            nc.vector.tensor_tensor(ssum[t][:, cols(h)], ex_t[t][:].indirect(half(n1_l, h)), ex2[t // 2][:, t % 2, cols(h)], ALU.add)

        z2_bf = keep.tile([P, 4 * S], BF16, name="z2_bf", tag="z2_bf", align_bytes=64)
        ssum = [keep.tile([P, S], F32, name="ssum0")[:]]

        def scale_z2(b):
            nc.vector.tensor_tensor(
                z2_bf[:, b * S : (b + 1) * S].rearrange("p (j t) -> p j t", t=4),
                back[b][:].rearrange("p (t j) -> p j t", t=4),
                gs_sb[:].unsqueeze(1).to_broadcast([P, P, 4]),
                ALU.mult,
            )

        def quantize_half(w, s, bf, h):
            nc.vector.quantize_mx(w[:, cols(h)].bitcast(FP8X4), s[:, cols(h)], bf[:, h * 4 * HALF : (h + 1) * 4 * HALF])

        scale_z2(0)
        scale_z2(1)
        for h in range(2):
            fetch_ex(0, h)
        weave(z2_bf[:, 4 * HALF :], absu[:], gs_sb)
        nc.vector.quantize_mx(z2_w[:].bitcast(FP8X4), z2_s[:], z2_bf[:])
        ssum.append(keep.tile([P, S], F32, name="ssum1", tag="absu")[:])
        ssum23 = keep.tile([P, 2, S], F32, name="ssum23", tag="z2_bf", align_bytes=64)
        ssum.extend([ssum23[:, 0, :], ssum23[:, 1, :]])
        for t in range(1, 4):
            for h in range(2):
                fetch_ex(t, h)
        lg = [keep.tile([P, 2, S], F32, name="lg%d" % i) for i in range(2)]

        def log_of(t):
            nc.scalar.activation(lg[t // 2][:, t % 2, :], ssum[t], ACT.Ln)

        log_of(0)

        b_ps = [product("bank%d" % (4 + m), xc_w, xc_s, m, z2_w, z2_s) for m in range(4)]

        w2_bf = keep.tile([P, 4 * S], BF16, name="w2_bf", tag="ex_again1", align_bytes=64)
        nc.vector.tensor_copy(w2_bf[:].rearrange("p (c i j) -> p c j i", i=4, j=4), w2_raw[:].rearrange("p j (c i) -> p c j i", i=4))
        w2_w, w2_s = mx_tiles("w2q")

        lnd = [keep.tile([P, 2, S], F32, name="lnd%d" % i, tag="lnd%d" % i) for i in range(2)]
        den = []

        def log_den(m):
            nc.scalar.activation(lnd[m // 2][:, m % 2, :], den[m][:], ACT.Ln, bias=0.5)

        for m in range(4):
            c = keep.tile([P, S], F32, name="c%d" % m)
            nc.scalar.activation(c[:], b_ps[m][:], ACT.Abs, scale=0.0625)
            if m < 2:
                log_of(2 * m + 1)
            g6 = keep.tile([P, S], F32, name="g6", tag="g6_%d" % m)
            for h in range(2):
                nc.scalar.activation(g6[:, cols(h)], c[:].indirect(half(n6_l, h)), ACT.Copy)
            den.append(bank(m))
            for b in range(4):
                turn(den[m][:, blk(b)], [c[:, blk(b)], g6[:, blk(b)]])
            if m == 0:
                log_of(2)
            if m > 0:
                log_den(m - 1)
        log_den(3)
        rec = [keep.tile([P, 2, S], F32, name="rec0", tag="g6_3"), keep.tile([P, 2, S], F32, name="rec1")]
        for i in range(2):
            nc.scalar.activation(rec[i][:], lnd[i][:], ACT.Exp, scale=-1.0)

        zf = keep.tile([P, 4, S], F32, name="zf")
        z_w, z_s = mx_tiles("zq")
        z_bf = keep.tile([P, 4 * S], BF16, name="z_bf", align_bytes=64)

        def fetch_y(t, h):
            nc.vector.tensor_tensor(zf[:, t, cols(h)], y_t[t][:].indirect(half(n2_l, h)), lg[t // 2][:, t % 2, cols(h)], ALU.subtract)

        def scale_z(h):
            weave(z_bf[:, h * 4 * HALF : (h + 1) * 4 * HALF], zf[:, :, cols(h)], ngn)

        fetch_y(0, 0)
        nc.vector.quantize_mx(w2_w[:].bitcast(FP8X4), w2_s[:], w2_bf[:])
        fetch_y(0, 1)
        fetch_y(1, 0)
        fetch_y(1, 1)
        fetch_y(2, 0)
        fetch_y(3, 0)
        fetch_y(2, 1)
        scale_z(0)
        fetch_y(3, 1)
        quantize_half(z_w, z_s, z_bf, 0)
        scale_z(1)
        quantize_half(z_w, z_s, z_bf, 1)

        a_ps = [product("bank%d" % (4 + m), w2_w, w2_s, m, z_w, z_s) for m in range(4)]
        a_t = []
        for m in range(4):
            a = keep.tile([P, S], F32, name="a%d" % m, tag=("lnd0" if m == 3 else "a%d" % m))
            if m < 3:
                nc.vector.tensor_copy(a[:], a_ps[m][:])
            a_t.append(a)
        late = keep.tile([P, 2, S], F32, name="late", tag="lnd1")
        for m in range(4):
            if m in (1, 2):
                g5 = late[:, m - 1, :]
            else:
                g5 = keep.tile([P, S], F32, name="g5_%d" % m)[:]
            if m == 3:
                nc.scalar.copy(a_t[m][:], a_ps[m][:])
            for h in range(2):
                if m == 0:
                    nc.vector.tensor_copy(g5[:, cols(h)], a_t[m][:].indirect(half(n5_l, h)))
                else:
                    nc.scalar.activation(g5[:, cols(h)], a_t[m][:].indirect(half(n5_l, h)), ACT.Copy)
            num = keep.tile([P, S], F32, name="num%d" % m)
            if m < 3:
                nc.gpsimd.tensor_tensor(num[:], a_t[m][:], g5, ALU.subtract)
            else:
                nc.vector.tensor_tensor(num[:], a_ps[m][:], g5, ALU.subtract)
            rb = bank(m)
            for b in range(4):
                turn(rb[:, blk(b)], [rec[m // 2][:, m % 2, blk(b)]])
            res = work.tile([P, S], F32, name="res", bufs=4)
            if m < 3:
                nc.vector.tensor_tensor(res[:], rb[:], num[:], ALU.mult)
                nc.sync.dma_start(out[m * P : (m + 1) * P, :], res[:])
            else:
                for h in range(2):
                    nc.vector.tensor_tensor(res[:, cols(h)], rb[:, cols(h)], num[:, cols(h)], ALU.mult)
                    queue = nc.sync if h == 0 else nc.scalar
                    queue.dma_start(out[m * P : (m + 1) * P, cols(h)], res[:, cols(h)])
